import numpy as np
import ml_dtypes


def mxq(x, axis, fmt="e4m3"):
    dtype, down = {"e4m3": (ml_dtypes.float8_e4m3fn, 7), "e5m2": (ml_dtypes.float8_e5m2, 14)}[fmt]
    v = np.moveaxis(np.asarray(x, np.float32).astype(ml_dtypes.bfloat16).astype(np.float64), axis, -1)
    blocks = v.reshape(v.shape[:-1] + (-1, 32))
    amax = np.abs(blocks).max(-1, keepdims=True)
    byte = np.maximum(np.where(amax > 0, np.frexp(amax)[1] - 1 + 127, 0) - down, 1)
    scale = np.exp2(byte - 127.0)
    codes = (blocks / scale).astype(np.float32).astype(dtype).astype(np.float64)
    return np.moveaxis((codes * scale).reshape(v.shape), -1, axis)


WIDE = False


def mx_kscale(k):
    if not WIDE:
        return np.ones(k)
    levels = np.array([10, -10, 5, -5, 0])
    if k % 512:
        return np.exp2(np.random.permutation(np.resize(levels, k // 32))).repeat(32)
    a = np.empty((k // 512, 16))
    for p in range(k // 512):
        a[p, :8] = np.random.permutation(np.resize(levels, 8))
        for g in range(8):
            far = levels[np.abs(levels - a[p, g]) >= 10]
            a[p, g + 8] = far[np.random.randint(len(far))]
    return np.exp2(a.ravel()).repeat(32)


def f64(x):
    return np.asarray(x).astype(np.float64)


def striped(idx):
    return np.tile(idx.reshape(-1, 16).T, (8, 1)).astype(np.uint16)


def unstriped(offs):
    return offs[:16].T.reshape(-1).astype(np.int64)


def pack_weight(w):
    k, n = w.shape
    w = f64(np.asarray(w, np.float32).astype(ml_dtypes.bfloat16)).reshape(k // 32, 32, n)
    amax = np.abs(w).max(1)
    byte = np.clip(np.where(amax > 0, np.frexp(amax)[1] - 1 + 127 - 7, 1), 1, 254)
    scaled = (w * np.exp2(127.0 - byte)[:, None, :]).reshape(k, n).astype(np.float32)
    words = np.ascontiguousarray(scaled.reshape(k // 512, 128, 4, n).transpose(0, 1, 3, 2)).astype(ml_dtypes.float8_e4m3fn).view(np.uint8)
    return words, np.ascontiguousarray(byte.astype(np.uint8).reshape(k // 512, 16, n))


def unpack_weight(words, scales):
    g, p, n, _ = words.shape
    vals = np.ascontiguousarray(words).view(ml_dtypes.float8_e4m3fn).astype(np.float64) * np.repeat(np.exp2(scales.astype(np.float64) - 127.0), 8, axis=1)[..., None]
    return vals.transpose(0, 1, 3, 2).reshape(g * 512, n)


def sigmoid(v):
    return 1.0 / (1.0 + np.exp(-np.maximum(v, -700.0)))


K, T, S, V = 512, 2048, 512, 512
P = 2 ** 7


def setup_inputs():
    n = np.random.standard_normal
    s = mx_kscale(K)[:, None]
    packed_xT = pack_weight(n((K, T)) * s)
    return {
        "x_words": packed_xT[0],
        "x_scales": packed_xT[1],
        "hT": (n((K, V)) / np.sqrt(K) / s).astype(np.float32),
        "diff": (np.tile(0.7 * n(T), (P, 1))).astype(np.float32),
        "guess": (np.tile(np.random.uniform(0.05, 0.3, T), (P, 1))).astype(np.float32),
        "offs": striped(np.random.permutation(T)[:S]),
    }


def reference(x_words, x_scales, hT, diff, guess, offs):
    gs = f64(guess)[:1][:, unstriped(offs)]
    hTq = mxq(f64(hT), 0, "e4m3")
    xq = unpack_weight(x_words, x_scales)[:, unstriped(offs)]
    y = (hTq.T @ xq) - (f64(diff)[:1][:, unstriped(offs)])
    sg = sigmoid(1.3 * y)
    prob = gs + (-1.0 * gs + 1.0) * sg
    return 10.0 * (((((-1.0 * gs + 1.0) * sg) * (-1.0 * sg + 1.0)) ** 2) / (prob * (-1.0 * (0.99 * prob) + 1.0)))

@@ -1,0 +1,174 @@
+from contextlib import ExitStack
+
+import concourse.mybir as mybir
+from concourse.masks import make_identity
+
+K, T, S, V = 512, 2048, 512, 512
+FLOPS = 2 * K * S * V
+BYTES = K * T + 16 * T + 4 * K * V + 2 * 4 * T + 128 * 32 * 2 + 4 * S * V
+
+F32 = mybir.dt.float32
+BF16 = mybir.dt.bfloat16
+I32 = mybir.dt.int32
+U32 = mybir.dt.uint32
+U16 = mybir.dt.uint16
+U8 = mybir.dt.uint8
+FP8X4 = mybir.dt.float8_e4m3fn_x4
+ALU = mybir.AluOpType
+ACT = mybir.ActivationFunctionType
+
+P = 128
+PACK = 4
+HALF = 256
+HALF_SLOPE = 0.65
+OUT_FACTOR = -250.0 / 99.0
+LN_FLOOR = 2.0 ** -60
+ROW_A, ROW_B, ROW_D = 8, 44, 80
+UNITS = [(b, h * HALF, HALF) for h in range(2) for b in range(4)]
+
+
+def tile_picked_yirt3_info_p_kernel(tc, x_words, x_scales, hT, diff, guess, offs, out):
+    nc = tc.nc
+    with ExitStack() as ctx:
+        keep = ctx.enter_context(tc.tile_pool(name="keep", bufs=1))
+        reuse = ctx.enter_context(tc.tile_pool(name="reuse", bufs=1))
+        psum = ctx.enter_context(tc.psum_pool(name="psum", bufs=1))
+
+        offsets = keep.tile([P, S // 16], U16, name="offsets")
+        nc.sync.dma_start(offsets[:], offs)
+
+        word_table = keep.tile([P, T], U32, name="word_table")
+        nc.sync.dma_start(out=word_table[:].bitcast(I32), in_=x_words[0].rearrange("p n t -> p (n t)").bitcast(I32))
+
+        h_rows = hT.rearrange("(p j) t -> p j t", j=PACK)
+        h_raw0 = keep.tile([P, PACK, HALF], F32, name="h_raw0")
+        nc.sync.dma_start(out=h_raw0[:], in_=h_rows[:, :, 0:HALF])
+
+        item_table = reuse.tile([P, T], F32, name="item_table", offset=0, align_bytes=64)
+        nc.vector.memset(item_table[:].bitcast(I32), 0)
+        nc.scalar.dma_start(out=item_table[ROW_A : ROW_B + 1 : ROW_B - ROW_A, :], in_=guess[0:2, :])
+        nc.scalar.dma_start(out=item_table[ROW_D : ROW_D + 1, :], in_=diff[0:1, :])
+
+        scale_table = keep.tile([P, T], U8, name="scale_table")
+        nc.vector.memset(scale_table[:].bitcast(I32), 0)
+        for q in range(4):
+            nc.scalar.dma_start(out=scale_table[32 * q : 32 * q + 4, :].bitcast(I32), in_=x_scales[0, 4 * q : 4 * q + 4, :].bitcast(I32))
+
+        ln_scale = keep.tile([P, 1], F32, name="ln_scale")
+        ln_bias = keep.tile([P, 1], F32, name="ln_bias")
+        for rows, scale, bias in ((slice(0, 32), 1.0, LN_FLOOR), (slice(32, 64), -99.0, 100.0), (slice(64, P), 0.0, 1.0)):
+            nc.gpsimd.memset(ln_scale[rows, :], scale)
+            nc.gpsimd.memset(ln_bias[rows, :], bias)
+
+        ident = keep.tile([P, P], F32, name="ident")
+        make_identity(nc, ident[:])
+
+        def list_half(h):
+            return offsets[:, h * (HALF // 16) : (h + 1) * (HALF // 16)]
+
+        picked = [keep.tile([P, HALF], F32, name=f"picked{h}") for h in range(2)]
+        logs = [keep.tile([P, HALF], F32, name=f"logs{h}") for h in range(2)]
+        picked_t = psum.tile([P, 4, P], F32, name="picked_t", tag="sum_a", bufs=2)
+        logs_t = psum.tile([P, 4, P], F32, name="logs_t", tag="sum_b", bufs=2)
+        for h in range(2):
+            nc.vector.tensor_copy(picked[h][:], item_table[:].indirect(list_half(h)))
+            nc.scalar.activation(logs[h][:], picked[h][:], ACT.Ln, bias=ln_bias[:], scale=ln_scale[:])
+        for src, dst in ((picked, picked_t), (logs, logs_t)):
+            for b in range(4):
+                nc.tensor.transpose(dst[:, b, :], src[b // 2][:, (b % 2) * P : (b % 2 + 1) * P], ident[:])
+
+        h_codes = keep.tile([P, V], U32, name="h_codes", align_bytes=64)
+        h_scales = keep.tile([P, V], U8, name="h_scales", align_bytes=64)
+        x_codes = [reuse.tile([P, HALF], U32, name=f"x_codes{h}", offset=1024 * h, align_bytes=64) for h in range(2)]
+        x_bytes = [reuse.tile([P, HALF], U8, name=f"x_bytes{h}", offset=2048 + 256 * h, align_bytes=64) for h in range(2)]
+        h_bf0 = reuse.tile([P, HALF, PACK], BF16, name="h_bf0", offset=2560, align_bytes=64)
+        h_bf1 = keep.tile([P, HALF, PACK], BF16, name="h_bf1", align_bytes=64)
+        h_bf = [h_bf0, h_bf1]
+        h_raw1 = reuse.tile([P, PACK, HALF], F32, name="h_raw1", offset=4608, align_bytes=64)
+        nc.sync.dma_start(out=h_raw1[:], in_=h_rows[:, :, HALF:V])
+        h_raw = [h_raw0, h_raw1]
+
+        def round_h(h):
+            nc.vector.tensor_copy(
+                out=h_bf[h][:].rearrange("p (c i) j -> p c j i", i=4),
+                in_=h_raw[h][:].rearrange("p j (c i) -> p c j i", i=4),
+            )
+
+        def quantize_h(h):
+            cols = slice(h * HALF, (h + 1) * HALF)
+            nc.vector.quantize_mx(
+                out=h_codes[:, cols].bitcast(FP8X4), scales=h_scales[:, cols], in_=h_bf[h][:].rearrange("p w j -> p (w j)")
+            )
+
+        def gather_scales(h):
+            nc.vector.tensor_copy(x_bytes[h][:], scale_table[:].indirect(list_half(h)))
+
+        def gather_words(h):
+            nc.vector.tensor_copy(x_codes[h][:], word_table[:].indirect(list_half(h)))
+
+        gather_scales(0)
+        gather_words(0)
+        round_h(0)
+
+        bias_n = keep.tile([P, 4], F32, name="bias_n")
+        bias_a = keep.tile([P, 4], F32, name="bias_a")
+        bias_b = keep.tile([P, 4], F32, name="bias_b")
+        nc.vector.tensor_scalar(bias_n[:], picked_t[:, :, ROW_D], HALF_SLOPE, None, ALU.mult)
+        nc.vector.scalar_tensor_tensor(bias_b[:], logs_t[:, :, ROW_B], -0.5, bias_n[:], ALU.mult, ALU.subtract)
+        nc.vector.scalar_tensor_tensor(bias_a[:], logs_t[:, :, ROW_A], -0.5, bias_n[:], ALU.mult, ALU.subtract)
+        quantize_h(0)
+        gather_scales(1)
+        gather_words(1)
+        round_h(1)
+        quantize_h(1)
+
+        out_rows = out.rearrange("(c p) j -> p c j", p=P)
+
+        def product(u):
+            b, t0, n = UNITS[u]
+            items = slice((b % 2) * P, (b % 2 + 1) * P)
+            score = psum.tile([P, n], F32, name="score", tag="score", bufs=4)
+            nc.tensor.matmul_mx(
+                out=score[:],
+                lhsT=x_codes[b // 2][:, items].bitcast(FP8X4),
+                lhsT_scale=x_bytes[b // 2][:, items],
+                rhs=h_codes[:, t0 : t0 + n].bitcast(FP8X4),
+                rhs_scale=h_scales[:, t0 : t0 + n],
+                start=True,
+                stop=True,
+            )
+            return score
+
+        def turn(dst, src, chunks, start, stop):
+            for c in range(chunks):
+                nc.tensor.matmul(
+                    dst[:, c, :], src[:, c * P : (c + 1) * P], ident[:],
+                    start=start and c == 0, stop=stop and c == chunks - 1, is_transpose=True,
+                )
+
+        def finish(u, score):
+            b, t0, n = UNITS[u]
+            chunks = n // P
+            tanh_n = keep.tile([P, n], F32, name=f"tanh_n{u}")
+            tanh_b = keep.tile([P, n], F32, name=f"tanh_b{u}")
+            tanh_a = keep.tile([P, n], F32, name=f"tanh_a{u}")
+            sum_b = psum.tile([P, chunks, P], F32, name="sum_b", tag="sum_b", bufs=2)
+            sum_a = psum.tile([P, chunks, P], F32, name="sum_a", tag="sum_a", bufs=2)
+            nc.scalar.activation(tanh_n[:], score[:], ACT.Tanh, bias=bias_n[:, b : b + 1], scale=-HALF_SLOPE)
+            turn(sum_b, tanh_n, chunks, True, False)
+            nc.scalar.activation(tanh_b[:], score[:], ACT.Tanh, bias=bias_b[:, b : b + 1], scale=HALF_SLOPE)
+            turn(sum_b, tanh_b, chunks, False, True)
+            turn(sum_a, tanh_n, chunks, True, False)
+            nc.scalar.activation(tanh_a[:], score[:], ACT.Tanh, bias=bias_a[:, b : b + 1], scale=HALF_SLOPE)
+            turn(sum_a, tanh_a, chunks, False, True)
+            factor_b = keep.tile([P, chunks, P], F32, name=f"factor_b{u}")
+            nc.vector.tensor_copy(factor_b[:], sum_b[:])
+            result = keep.tile([P, chunks, P], F32, name=f"result{u}")
+            nc.vector.scalar_tensor_tensor(result[:], sum_a[:], OUT_FACTOR, factor_b[:], ALU.mult, ALU.mult)
+            nc.sync.dma_start(out=out_rows[:, t0 // P : t0 // P + chunks, b * P : (b + 1) * P], in_=result[:])
+
+        scores = [product(0), product(1)]
+        for u in range(len(UNITS)):
+            if u + 2 < len(UNITS):
+                scores.append(product(u + 2))
+            finish(u, scores[u])

@@ -37,28 +37,31 @@ def tile_picked_yirt3_info_p_kernel(tc, x_words, x_scales, hT, diff, guess, offs
         offsets = keep.tile([P, S // 16], U16, name="offsets")
         nc.sync.dma_start(offsets[:], offs)
 
-        word_table = keep.tile([P, T], U32, name="word_table")
-        nc.sync.dma_start(out=word_table[:].bitcast(I32), in_=x_words[0].rearrange("p n t -> p (n t)").bitcast(I32))
-
         h_rows = hT.rearrange("(p j) t -> p j t", j=PACK)
         h_raw0 = keep.tile([P, PACK, HALF], F32, name="h_raw0")
-        nc.sync.dma_start(out=h_raw0[:], in_=h_rows[:, :, 0:HALF])
+        nc.scalar.dma_start(out=h_raw0[:], in_=h_rows[:, :, 0:HALF])
+
+        word_table = keep.tile([P, T], U32, name="word_table")
+        nc.scalar.dma_start(out=word_table[:].bitcast(I32), in_=x_words[0].rearrange("p n t -> p (n t)").bitcast(I32))
 
         item_table = reuse.tile([P, T], F32, name="item_table", offset=0, align_bytes=64)
         nc.vector.memset(item_table[:].bitcast(I32), 0)
-        nc.scalar.dma_start(out=item_table[ROW_A : ROW_B + 1 : ROW_B - ROW_A, :], in_=guess[0:2, :])
-        nc.scalar.dma_start(out=item_table[ROW_D : ROW_D + 1, :], in_=diff[0:1, :])
+        nc.sync.dma_start(out=item_table[ROW_A : ROW_B + 1 : ROW_B - ROW_A, :], in_=guess[0:2, :])
+        nc.sync.dma_start(out=item_table[ROW_D : ROW_D + 1, :], in_=diff[0:1, :])
 
         scale_table = keep.tile([P, T], U8, name="scale_table")
         nc.vector.memset(scale_table[:].bitcast(I32), 0)
         for q in range(4):
-            nc.scalar.dma_start(out=scale_table[32 * q : 32 * q + 4, :].bitcast(I32), in_=x_scales[0, 4 * q : 4 * q + 4, :].bitcast(I32))
+            nc.sync.dma_start(out=scale_table[32 * q : 32 * q + 4, :].bitcast(I32), in_=x_scales[0, 4 * q : 4 * q + 4, :].bitcast(I32))
 
         ln_scale = keep.tile([P, 1], F32, name="ln_scale")
         ln_bias = keep.tile([P, 1], F32, name="ln_bias")
         for rows, scale, bias in ((slice(0, 32), 1.0, LN_FLOOR), (slice(32, 64), -99.0, 100.0), (slice(64, P), 0.0, 1.0)):
             nc.gpsimd.memset(ln_scale[rows, :], scale)
             nc.gpsimd.memset(ln_bias[rows, :], bias)
+
+        warm = keep.tile([P, 2], F32, name="warm")
+        nc.scalar.activation(warm[:, 0:1], ln_bias[:], ACT.Ln)
 
         ident = keep.tile([P, P], F32, name="ident")
         make_identity(nc, ident[:])
@@ -68,20 +71,21 @@ def tile_picked_yirt3_info_p_kernel(tc, x_words, x_scales, hT, diff, guess, offs
 
         picked = [keep.tile([P, HALF], F32, name=f"picked{h}") for h in range(2)]
         logs = [keep.tile([P, HALF], F32, name=f"logs{h}") for h in range(2)]
-        picked_t = psum.tile([P, 4, P], F32, name="picked_t", tag="sum_a", bufs=2)
-        logs_t = psum.tile([P, 4, P], F32, name="logs_t", tag="sum_b", bufs=2)
+        picked_t = psum.tile([P, 4, P], F32, name="picked_t", tag="sums", bufs=4)
+        logs_t = psum.tile([P, 4, P], F32, name="logs_t", tag="sums", bufs=4)
         for h in range(2):
             nc.vector.tensor_copy(picked[h][:], item_table[:].indirect(list_half(h)))
             nc.scalar.activation(logs[h][:], picked[h][:], ACT.Ln, bias=ln_bias[:], scale=ln_scale[:])
+        nc.scalar.activation(warm[:, 1:2], logs[1][:, 0:1], ACT.Tanh)
         for src, dst in ((picked, picked_t), (logs, logs_t)):
             for b in range(4):
                 nc.tensor.transpose(dst[:, b, :], src[b // 2][:, (b % 2) * P : (b % 2 + 1) * P], ident[:])
 
-        h_codes = keep.tile([P, V], U32, name="h_codes", align_bytes=64)
+        h_codes = reuse.tile([P, V], U32, name="h_codes", offset=2560, align_bytes=64)
         h_scales = keep.tile([P, V], U8, name="h_scales", align_bytes=64)
         x_codes = [reuse.tile([P, HALF], U32, name=f"x_codes{h}", offset=1024 * h, align_bytes=64) for h in range(2)]
         x_bytes = [reuse.tile([P, HALF], U8, name=f"x_bytes{h}", offset=2048 + 256 * h, align_bytes=64) for h in range(2)]
-        h_bf0 = reuse.tile([P, HALF, PACK], BF16, name="h_bf0", offset=2560, align_bytes=64)
+        h_bf0 = keep.tile([P, HALF, PACK], BF16, name="h_bf0", align_bytes=64)
         h_bf1 = keep.tile([P, HALF, PACK], BF16, name="h_bf1", align_bytes=64)
         h_bf = [h_bf0, h_bf1]
         h_raw1 = reuse.tile([P, PACK, HALF], F32, name="h_raw1", offset=4608, align_bytes=64)
@@ -89,10 +93,7 @@ def tile_picked_yirt3_info_p_kernel(tc, x_words, x_scales, hT, diff, guess, offs
         h_raw = [h_raw0, h_raw1]
 
         def round_h(h):
-            nc.vector.tensor_copy(
-                out=h_bf[h][:].rearrange("p (c i) j -> p c j i", i=4),
-                in_=h_raw[h][:].rearrange("p j (c i) -> p c j i", i=4),
-            )
+            nc.gpsimd.tensor_copy(out=h_bf[h][:], in_=h_raw[h][:].rearrange("p j w -> p w j"))
 
         def quantize_h(h):
             cols = slice(h * HALF, (h + 1) * HALF)
@@ -106,9 +107,10 @@ def tile_picked_yirt3_info_p_kernel(tc, x_words, x_scales, hT, diff, guess, offs
         def gather_words(h):
             nc.vector.tensor_copy(x_codes[h][:], word_table[:].indirect(list_half(h)))
 
-        gather_scales(0)
-        gather_words(0)
         round_h(0)
+        gather_scales(0)
+        quantize_h(0)
+        gather_words(0)
 
         bias_n = keep.tile([P, 4], F32, name="bias_n")
         bias_a = keep.tile([P, 4], F32, name="bias_a")
@@ -116,28 +118,31 @@ def tile_picked_yirt3_info_p_kernel(tc, x_words, x_scales, hT, diff, guess, offs
         nc.vector.tensor_scalar(bias_n[:], picked_t[:, :, ROW_D], HALF_SLOPE, None, ALU.mult)
         nc.vector.scalar_tensor_tensor(bias_b[:], logs_t[:, :, ROW_B], -0.5, bias_n[:], ALU.mult, ALU.subtract)
         nc.vector.scalar_tensor_tensor(bias_a[:], logs_t[:, :, ROW_A], -0.5, bias_n[:], ALU.mult, ALU.subtract)
-        quantize_h(0)
+        round_h(1)
         gather_scales(1)
         gather_words(1)
-        round_h(1)
         quantize_h(1)
 
         out_rows = out.rearrange("(c p) j -> p c j", p=P)
 
-        def product(u):
-            b, t0, n = UNITS[u]
-            items = slice((b % 2) * P, (b % 2 + 1) * P)
-            score = psum.tile([P, n], F32, name="score", tag="score", bufs=4)
-            nc.tensor.matmul_mx(
-                out=score[:],
-                lhsT=x_codes[b // 2][:, items].bitcast(FP8X4),
-                lhsT_scale=x_bytes[b // 2][:, items],
-                rhs=h_codes[:, t0 : t0 + n].bitcast(FP8X4),
-                rhs_scale=h_scales[:, t0 : t0 + n],
-                start=True,
-                stop=True,
-            )
-            return score
+        def products(units):
+            bank = psum.tile([P, 2 * HALF], F32, name="score", tag="score", bufs=4)
+            views = []
+            for i, u in enumerate(units):
+                b, t0, n = UNITS[u]
+                items = slice((b % 2) * P, (b % 2 + 1) * P)
+                view = bank[:, i * HALF : i * HALF + n]
+                nc.tensor.matmul_mx(
+                    out=view,
+                    lhsT=x_codes[b // 2][:, items].bitcast(FP8X4),
+                    lhsT_scale=x_bytes[b // 2][:, items],
+                    rhs=h_codes[:, t0 : t0 + n].bitcast(FP8X4),
+                    rhs_scale=h_scales[:, t0 : t0 + n],
+                    start=True,
+                    stop=True,
+                )
+                views.append(view)
+            return views
 
         def turn(dst, src, chunks, start, stop):
             for c in range(chunks):
@@ -146,29 +151,38 @@ def tile_picked_yirt3_info_p_kernel(tc, x_words, x_scales, hT, diff, guess, offs
                     start=start and c == 0, stop=stop and c == chunks - 1, is_transpose=True,
                 )
 
-        def finish(u, score):
-            b, t0, n = UNITS[u]
+        def finish(name, b, t0, score, apart):
+            n = score.shape[1]
             chunks = n // P
-            tanh_n = keep.tile([P, n], F32, name=f"tanh_n{u}")
-            tanh_b = keep.tile([P, n], F32, name=f"tanh_b{u}")
-            tanh_a = keep.tile([P, n], F32, name=f"tanh_a{u}")
-            sum_b = psum.tile([P, chunks, P], F32, name="sum_b", tag="sum_b", bufs=2)
-            sum_a = psum.tile([P, chunks, P], F32, name="sum_a", tag="sum_a", bufs=2)
-            nc.scalar.activation(tanh_n[:], score[:], ACT.Tanh, bias=bias_n[:, b : b + 1], scale=-HALF_SLOPE)
+            tanh_n = keep.tile([P, n], F32, name=f"tanh_n{name}")
+            tanh_b = keep.tile([P, n], F32, name=f"tanh_b{name}")
+            tanh_a = keep.tile([P, n], F32, name=f"tanh_a{name}")
+            if apart:
+                bank_b = psum.tile([P, chunks, P], F32, name="bank_b", tag="sums", bufs=4)
+                bank_a = psum.tile([P, chunks, P], F32, name="bank_a", tag="sums", bufs=4)
+                sum_b, sum_a = bank_b[:], bank_a[:]
+            else:
+                bank = psum.tile([P, 2, chunks, P], F32, name="bank", tag="sums", bufs=4)
+                sum_b, sum_a = bank[:, 0, :, :], bank[:, 1, :, :]
+            nc.scalar.activation(tanh_n[:], score, ACT.Tanh, bias=bias_n[:, b : b + 1], scale=-HALF_SLOPE)
             turn(sum_b, tanh_n, chunks, True, False)
-            nc.scalar.activation(tanh_b[:], score[:], ACT.Tanh, bias=bias_b[:, b : b + 1], scale=HALF_SLOPE)
-            turn(sum_b, tanh_b, chunks, False, True)
-            turn(sum_a, tanh_n, chunks, True, False)
-            nc.scalar.activation(tanh_a[:], score[:], ACT.Tanh, bias=bias_a[:, b : b + 1], scale=HALF_SLOPE)
+            turn(sum_a, tanh_n, chunks, apart, False)
+            nc.scalar.activation(tanh_b[:], score, ACT.Tanh, bias=bias_b[:, b : b + 1], scale=HALF_SLOPE)
+            turn(sum_b, tanh_b, chunks, False, apart)
+            nc.scalar.activation(tanh_a[:], score, ACT.Tanh, bias=bias_a[:, b : b + 1], scale=HALF_SLOPE)
             turn(sum_a, tanh_a, chunks, False, True)
-            factor_b = keep.tile([P, chunks, P], F32, name=f"factor_b{u}")
-            nc.vector.tensor_copy(factor_b[:], sum_b[:])
-            result = keep.tile([P, chunks, P], F32, name=f"result{u}")
-            nc.vector.scalar_tensor_tensor(result[:], sum_a[:], OUT_FACTOR, factor_b[:], ALU.mult, ALU.mult)
+            factor_b = keep.tile([P, chunks, P], F32, name=f"factor_b{name}")
+            nc.vector.tensor_copy(factor_b[:], sum_b)
+            result = keep.tile([P, chunks, P], F32, name=f"result{name}")
+            nc.vector.scalar_tensor_tensor(result[:], sum_a, OUT_FACTOR, factor_b[:], ALU.mult, ALU.mult)
             nc.sync.dma_start(out=out_rows[:, t0 // P : t0 // P + chunks, b * P : (b + 1) * P], in_=result[:])
 
-        scores = [product(0), product(1)]
-        for u in range(len(UNITS)):
-            if u + 2 < len(UNITS):
-                scores.append(product(u + 2))
-            finish(u, scores[u])
+        scores = products([0]) + products([1])
+        finish("0", 0, 0, scores[0], False)
+        scores = scores + products([2, 3])
+        finish("1", 1, 0, scores[1], False)
+        scores = scores + products([4, 5]) + products([6, 7])
+        for u in range(2, len(UNITS) - 1):
+            finish(str(u), UNITS[u][0], UNITS[u][1], scores[u], False)
+        finish("7a", 3, HALF, scores[7][:, 0:P], True)
+        finish("7b", 3, HALF + P, scores[7][:, P:HALF], True)

@@ -39,29 +39,40 @@ def tile_picked_yirt3_info_p_kernel(tc, x_words, x_scales, hT, diff, guess, offs
 
         h_rows = hT.rearrange("(p j) t -> p j t", j=PACK)
         h_raw0 = keep.tile([P, PACK, HALF], F32, name="h_raw0")
-        nc.scalar.dma_start(out=h_raw0[:], in_=h_rows[:, :, 0:HALF])
+        nc.sync.dma_start(out=h_raw0[:], in_=h_rows[:, :, 0:HALF])
 
-        word_table = keep.tile([P, T], U32, name="word_table")
-        nc.scalar.dma_start(out=word_table[:].bitcast(I32), in_=x_words[0].rearrange("p n t -> p (n t)").bitcast(I32))
-
-        item_table = reuse.tile([P, T], F32, name="item_table", offset=0, align_bytes=64)
-        nc.vector.memset(item_table[:].bitcast(I32), 0)
-        nc.sync.dma_start(out=item_table[ROW_A : ROW_B + 1 : ROW_B - ROW_A, :], in_=guess[0:2, :])
-        nc.sync.dma_start(out=item_table[ROW_D : ROW_D + 1, :], in_=diff[0:1, :])
+        one = reuse.tile([P, 32], F32, name="one", offset=12352, align_bytes=64)
+        warm = keep.tile([P, 2], F32, name="warm")
+        nc.vector.memset(one[:, 0:1], 1.0)
+        nc.scalar.activation(warm[:, 0:1], one[:, 0:1], ACT.Ln)
 
         scale_table = keep.tile([P, T], U8, name="scale_table")
         nc.vector.memset(scale_table[:].bitcast(I32), 0)
+
+        def load_scales(queue, q):
+            queue.dma_start(out=scale_table[32 * q : 32 * q + 4, :].bitcast(I32), in_=x_scales[0, 4 * q : 4 * q + 4, :].bitcast(I32))
+
         for q in range(4):
-            nc.sync.dma_start(out=scale_table[32 * q : 32 * q + 4, :].bitcast(I32), in_=x_scales[0, 4 * q : 4 * q + 4, :].bitcast(I32))
+            load_scales(nc.sync, q)
+
+        item_table = reuse.tile([P, T + 16], F32, name="item_table", offset=0, align_bytes=64)
+        nc.vector.memset(item_table[:].bitcast(I32), 0)
+        nc.sync.dma_start(out=item_table[ROW_A : ROW_B + 1 : ROW_B - ROW_A, 0:T], in_=guess[0:2, :])
+        nc.sync.dma_start(out=item_table[ROW_D : ROW_D + 1, 0:T], in_=diff[0:1, :])
 
         ln_scale = keep.tile([P, 1], F32, name="ln_scale")
         ln_bias = keep.tile([P, 1], F32, name="ln_bias")
-        for rows, scale, bias in ((slice(0, 32), 1.0, LN_FLOOR), (slice(32, 64), -99.0, 100.0), (slice(64, P), 0.0, 1.0)):
-            nc.gpsimd.memset(ln_scale[rows, :], scale)
-            nc.gpsimd.memset(ln_bias[rows, :], bias)
+        nc.gpsimd.memset(ln_scale[0:32, :], 1.0)
+        nc.gpsimd.memset(ln_scale[32:64, :], -99.0)
+        nc.gpsimd.memset(ln_scale[64:P, :], 0.0)
+        nc.gpsimd.memset(ln_bias[0:32, :], LN_FLOOR)
+        nc.gpsimd.memset(ln_bias[32:64, :], 100.0)
+        nc.vector.tensor_tensor(ln_bias[64:P, :], one[64:P, 0:1], item_table[64:P, T : T + 1], ALU.add)
 
-        warm = keep.tile([P, 2], F32, name="warm")
-        nc.scalar.activation(warm[:, 0:1], ln_bias[:], ACT.Ln)
+        word_table = reuse.tile([P, T], U32, name="word_table", offset=12416, align_bytes=64)
+        nc.sync.dma_start(out=word_table[:].bitcast(I32), in_=x_words[0].rearrange("p n t -> p (n t)").bitcast(I32))
+        h_raw1 = reuse.tile([P, PACK, HALF], F32, name="h_raw1", offset=8320, align_bytes=64)
+        nc.sync.dma_start(out=h_raw1[:], in_=h_rows[:, :, HALF:V])
 
         ident = keep.tile([P, P], F32, name="ident")
         make_identity(nc, ident[:])
@@ -71,29 +82,29 @@ def tile_picked_yirt3_info_p_kernel(tc, x_words, x_scales, hT, diff, guess, offs
 
         picked = [keep.tile([P, HALF], F32, name=f"picked{h}") for h in range(2)]
         logs = [keep.tile([P, HALF], F32, name=f"logs{h}") for h in range(2)]
-        picked_t = psum.tile([P, 4, P], F32, name="picked_t", tag="sums", bufs=4)
-        logs_t = psum.tile([P, 4, P], F32, name="logs_t", tag="sums", bufs=4)
+        turned = [psum.tile([P, 2, 2, P], F32, name=f"turned{h}", tag="sums", bufs=4) for h in range(2)]
         for h in range(2):
-            nc.vector.tensor_copy(picked[h][:], item_table[:].indirect(list_half(h)))
+            nc.vector.tensor_copy(picked[h][:], item_table[:, 0:T].indirect(list_half(h)))
             nc.scalar.activation(logs[h][:], picked[h][:], ACT.Ln, bias=ln_bias[:], scale=ln_scale[:])
+            for i, src in enumerate((picked[h], logs[h])):
+                for c in range(2):
+                    nc.tensor.transpose(turned[h][:, i, c, :], src[:, c * P : (c + 1) * P], ident[:])
         nc.scalar.activation(warm[:, 1:2], logs[1][:, 0:1], ACT.Tanh)
-        for src, dst in ((picked, picked_t), (logs, logs_t)):
-            for b in range(4):
-                nc.tensor.transpose(dst[:, b, :], src[b // 2][:, (b % 2) * P : (b % 2 + 1) * P], ident[:])
 
         h_codes = reuse.tile([P, V], U32, name="h_codes", offset=2560, align_bytes=64)
         h_scales = keep.tile([P, V], U8, name="h_scales", align_bytes=64)
         x_codes = [reuse.tile([P, HALF], U32, name=f"x_codes{h}", offset=1024 * h, align_bytes=64) for h in range(2)]
-        x_bytes = [reuse.tile([P, HALF], U8, name=f"x_bytes{h}", offset=2048 + 256 * h, align_bytes=64) for h in range(2)]
+        x_bytes = [reuse.tile([P, HALF], U8, name=f"x_bytes{h}", offset=(2048, 12416)[h], align_bytes=64) for h in range(2)]
         h_bf0 = keep.tile([P, HALF, PACK], BF16, name="h_bf0", align_bytes=64)
         h_bf1 = keep.tile([P, HALF, PACK], BF16, name="h_bf1", align_bytes=64)
         h_bf = [h_bf0, h_bf1]
-        h_raw1 = reuse.tile([P, PACK, HALF], F32, name="h_raw1", offset=4608, align_bytes=64)
-        nc.sync.dma_start(out=h_raw1[:], in_=h_rows[:, :, HALF:V])
         h_raw = [h_raw0, h_raw1]
 
         def round_h(h):
-            nc.gpsimd.tensor_copy(out=h_bf[h][:], in_=h_raw[h][:].rearrange("p j w -> p w j"))
+            nc.vector.tensor_copy(
+                out=h_bf[h][:].rearrange("p (c i) j -> p c j i", i=4),
+                in_=h_raw[h][:].rearrange("p j (c i) -> p c j i", i=4),
+            )
 
         def quantize_h(h):
             cols = slice(h * HALF, (h + 1) * HALF)
@@ -107,20 +118,25 @@ def tile_picked_yirt3_info_p_kernel(tc, x_words, x_scales, hT, diff, guess, offs
         def gather_words(h):
             nc.vector.tensor_copy(x_codes[h][:], word_table[:].indirect(list_half(h)))
 
-        round_h(0)
-        gather_scales(0)
-        quantize_h(0)
-        gather_words(0)
+        bias_n = [keep.tile([P, 2], F32, name="bias_n0"), reuse.tile([P, 2], F32, name="bias_n1", offset=12672, align_bytes=64)]
+        bias_ab = [keep.tile([P, 2, 2], F32, name="bias_ab0"), reuse.tile([P, 2, 2], F32, name="bias_ab1", offset=12736, align_bytes=64)]
 
-        bias_n = keep.tile([P, 4], F32, name="bias_n")
-        bias_a = keep.tile([P, 4], F32, name="bias_a")
-        bias_b = keep.tile([P, 4], F32, name="bias_b")
-        nc.vector.tensor_scalar(bias_n[:], picked_t[:, :, ROW_D], HALF_SLOPE, None, ALU.mult)
-        nc.vector.scalar_tensor_tensor(bias_b[:], logs_t[:, :, ROW_B], -0.5, bias_n[:], ALU.mult, ALU.subtract)
-        nc.vector.scalar_tensor_tensor(bias_a[:], logs_t[:, :, ROW_A], -0.5, bias_n[:], ALU.mult, ALU.subtract)
-        round_h(1)
-        gather_scales(1)
+        def biases(h):
+            nc.vector.tensor_scalar(bias_n[h][:], turned[h][:, 0, :, ROW_D], HALF_SLOPE, None, ALU.mult)
+            nc.vector.scalar_tensor_tensor(
+                bias_ab[h][:], turned[h][:, 1, :, ROW_A : ROW_B + 1 : ROW_B - ROW_A], -0.5,
+                bias_n[h][:].unsqueeze(2).to_broadcast([P, 2, 2]), ALU.mult, ALU.subtract,
+            )
+
+        round_h(0)
+        quantize_h(0)
+        gather_scales(0)
+        biases(0)
+        gather_words(0)
         gather_words(1)
+        gather_scales(1)
+        biases(1)
+        round_h(1)
         quantize_h(1)
 
         out_rows = out.rearrange("(c p) j -> p c j", p=P)
@@ -151,38 +167,112 @@ def tile_picked_yirt3_info_p_kernel(tc, x_words, x_scales, hT, diff, guess, offs
                     start=start and c == 0, stop=stop and c == chunks - 1, is_transpose=True,
                 )
 
-        def finish(name, b, t0, score, apart):
+        def tanh_tiles(name, n):
+            return [keep.tile([P, n], F32, name=f"tanh_{kind}{name}") for kind in ("n", "b", "a")]
+
+        def store(result, b, t0, chunks):
+            nc.sync.dma_start(out=out_rows[:, t0 // P : t0 // P + chunks, b * P : (b + 1) * P], in_=result[:])
+
+        def sums_on_tensor(name, b, t0, score, last):
             n = score.shape[1]
             chunks = n // P
-            tanh_n = keep.tile([P, n], F32, name=f"tanh_n{name}")
-            tanh_b = keep.tile([P, n], F32, name=f"tanh_b{name}")
-            tanh_a = keep.tile([P, n], F32, name=f"tanh_a{name}")
-            if apart:
-                bank_b = psum.tile([P, chunks, P], F32, name="bank_b", tag="sums", bufs=4)
+            tanh_n, tanh_b, tanh_a = tanh_tiles(name, n)
+            if last:
+                bank_b = psum.tile([P, chunks, P], F32, name="bank_b", tag="score", bufs=4)
                 bank_a = psum.tile([P, chunks, P], F32, name="bank_a", tag="sums", bufs=4)
                 sum_b, sum_a = bank_b[:], bank_a[:]
             else:
                 bank = psum.tile([P, 2, chunks, P], F32, name="bank", tag="sums", bufs=4)
                 sum_b, sum_a = bank[:, 0, :, :], bank[:, 1, :, :]
-            nc.scalar.activation(tanh_n[:], score, ACT.Tanh, bias=bias_n[:, b : b + 1], scale=-HALF_SLOPE)
+            nc.scalar.activation(tanh_n[:], score, ACT.Tanh, bias=bias_n[b // 2][:, b % 2 : b % 2 + 1], scale=-HALF_SLOPE)
             turn(sum_b, tanh_n, chunks, True, False)
-            turn(sum_a, tanh_n, chunks, apart, False)
-            nc.scalar.activation(tanh_b[:], score, ACT.Tanh, bias=bias_b[:, b : b + 1], scale=HALF_SLOPE)
-            turn(sum_b, tanh_b, chunks, False, apart)
-            nc.scalar.activation(tanh_a[:], score, ACT.Tanh, bias=bias_a[:, b : b + 1], scale=HALF_SLOPE)
+            turn(sum_a, tanh_n, chunks, last, False)
+            nc.scalar.activation(tanh_b[:], score, ACT.Tanh, bias=bias_ab[b // 2][:, b % 2, 1:2], scale=HALF_SLOPE)
+            turn(sum_b, tanh_b, chunks, False, last)
+            nc.scalar.activation(tanh_a[:], score, ACT.Tanh, bias=bias_ab[b // 2][:, b % 2, 0:1], scale=HALF_SLOPE)
             turn(sum_a, tanh_a, chunks, False, True)
-            factor_b = keep.tile([P, chunks, P], F32, name=f"factor_b{name}")
-            nc.vector.tensor_copy(factor_b[:], sum_b)
-            result = keep.tile([P, chunks, P], F32, name=f"result{name}")
-            nc.vector.scalar_tensor_tensor(result[:], sum_a, OUT_FACTOR, factor_b[:], ALU.mult, ALU.mult)
-            nc.sync.dma_start(out=out_rows[:, t0 // P : t0 // P + chunks, b * P : (b + 1) * P], in_=result[:])
+
+            def finish():
+                factor_b = keep.tile([P, chunks, P], F32, name=f"factor_b{name}")
+                if last:
+                    nc.scalar.copy(factor_b[:], sum_b)
+                else:
+                    nc.vector.tensor_copy(factor_b[:], sum_b)
+                result = keep.tile([P, chunks, P], F32, name=f"result{name}")
+                nc.vector.scalar_tensor_tensor(result[:], sum_a, OUT_FACTOR, factor_b[:], ALU.mult, ALU.mult)
+                store(result, b, t0, chunks)
+
+            return finish
+
+        def sums_shared(name, b, t0, score):
+            n = score.shape[1]
+            chunks = n // P
+            tanh_n, tanh_b, tanh_a = tanh_tiles(name, n)
+            sum_items = keep.tile([P, n], F32, name=f"sum_items{name}")
+            bank = psum.tile([P, 2, chunks, P], F32, name="bank", tag="sums", bufs=4)
+            sum_b, sum_a = bank[:, 0, :, :], bank[:, 1, :, :]
+            nc.scalar.activation(tanh_n[:], score, ACT.Tanh, bias=bias_n[b // 2][:, b % 2 : b % 2 + 1], scale=-HALF_SLOPE)
+            turn(sum_a, tanh_n, chunks, True, False)
+            nc.scalar.activation(tanh_b[:], score, ACT.Tanh, bias=bias_ab[b // 2][:, b % 2, 1:2], scale=HALF_SLOPE)
+            nc.gpsimd.tensor_tensor(sum_items[:], tanh_b[:], tanh_n[:], ALU.add)
+            nc.scalar.activation(tanh_a[:], score, ACT.Tanh, bias=bias_ab[b // 2][:, b % 2, 0:1], scale=HALF_SLOPE)
+            turn(sum_a, tanh_a, chunks, False, False)
+            turn(sum_b, sum_items, chunks, False, True)
+
+            def finish():
+                factor_b = keep.tile([P, chunks, P], F32, name=f"factor_b{name}")
+                nc.vector.tensor_copy(factor_b[:], sum_b)
+                result = keep.tile([P, chunks, P], F32, name=f"result{name}")
+                nc.vector.scalar_tensor_tensor(result[:], sum_a, OUT_FACTOR, factor_b[:], ALU.mult, ALU.mult)
+                store(result, b, t0, chunks)
+
+            return finish
+
+        def sums_on_vector(name, b, t0, score, between, copy_on_scalar):
+            n = score.shape[1]
+            chunks = n // P
+            tanh_n, tanh_b, tanh_a = tanh_tiles(name, n)
+            sum_b = keep.tile([P, n], F32, name=f"sum_b{name}")
+            sum_a = keep.tile([P, n], F32, name=f"sum_a{name}")
+            info = keep.tile([P, n], F32, name=f"info{name}")
+            nc.scalar.activation(tanh_n[:], score, ACT.Tanh, bias=bias_n[b // 2][:, b % 2 : b % 2 + 1], scale=-HALF_SLOPE)
+            nc.scalar.activation(tanh_b[:], score, ACT.Tanh, bias=bias_ab[b // 2][:, b % 2, 1:2], scale=HALF_SLOPE)
+            nc.scalar.activation(tanh_a[:], score, ACT.Tanh, bias=bias_ab[b // 2][:, b % 2, 0:1], scale=HALF_SLOPE)
+            nc.vector.tensor_tensor(sum_b[:], tanh_b[:], tanh_n[:], ALU.add)
+            nc.vector.tensor_tensor(sum_a[:], tanh_a[:], tanh_n[:], ALU.add)
+            between()
+            nc.vector.scalar_tensor_tensor(info[:], sum_a[:], OUT_FACTOR, sum_b[:], ALU.mult, ALU.mult)
+            bank = psum.tile([P, chunks, P], F32, name="bank", tag="sums", bufs=4)
+            turn(bank, info, chunks, True, True)
+
+            def finish():
+                result = keep.tile([P, chunks, P], F32, name=f"result{name}")
+                if copy_on_scalar:
+                    nc.scalar.copy(result[:], bank[:])
+                else:
+                    nc.vector.tensor_copy(result[:], bank[:])
+                store(result, b, t0, chunks)
+
+            return finish
 
         scores = products([0]) + products([1])
-        finish("0", 0, 0, scores[0], False)
+        f0 = sums_on_tensor("0", 0, 0, scores[0], False)
         scores = scores + products([2, 3])
-        finish("1", 1, 0, scores[1], False)
+        f1 = sums_on_tensor("1", 1, 0, scores[1], False)
+        f0()
         scores = scores + products([4, 5]) + products([6, 7])
-        for u in range(2, len(UNITS) - 1):
-            finish(str(u), UNITS[u][0], UNITS[u][1], scores[u], False)
-        finish("7a", 3, HALF, scores[7][:, 0:P], True)
-        finish("7b", 3, HALF + P, scores[7][:, P:HALF], True)
+        f2 = sums_on_tensor("2", 2, 0, scores[2], False)
+        f1()
+        f3 = sums_shared("3", 3, 0, scores[3])
+        f2()
+        f4 = sums_shared("4", 0, HALF, scores[4])
+        f3()
+        f5 = sums_shared("5", 1, HALF, scores[5])
+        f4()
+        f6 = sums_shared("6", 2, HALF, scores[6])
+        f5()
+        f7a = sums_on_tensor("7a", 3, HALF, scores[7][:, 0:P], True)
+        f6()
+        f7b = sums_on_tensor("7b", 3, HALF + P, scores[7][:, P:HALF], True)
+        f7a()
+        f7b()

from contextlib import ExitStack

import concourse.mybir as mybir
from concourse.masks import make_identity

K, T, S, V = 512, 2048, 512, 512
FLOPS = 2 * K * S * V
BYTES = K * T + 16 * T + 4 * K * V + 2 * 4 * T + 128 * 32 * 2 + 4 * S * V

F32 = mybir.dt.float32
BF16 = mybir.dt.bfloat16
I32 = mybir.dt.int32
U32 = mybir.dt.uint32
U16 = mybir.dt.uint16
U8 = mybir.dt.uint8
FP8X4 = mybir.dt.float8_e4m3fn_x4
ALU = mybir.AluOpType
ACT = mybir.ActivationFunctionType

P = 128
PACK = 4
HALF = 256
HALF_SLOPE = 0.65
OUT_FACTOR = -250.0 / 99.0
LN_FLOOR = 2.0 ** -60
ROW_A, ROW_B, ROW_D = 8, 44, 80
UNITS = [(b, h * HALF, HALF) for h in range(2) for b in range(4)]


def tile_picked_yirt3_info_p_kernel(tc, x_words, x_scales, hT, diff, guess, offs, out):
    nc = tc.nc
    with ExitStack() as ctx:
        keep = ctx.enter_context(tc.tile_pool(name="keep", bufs=1))
        reuse = ctx.enter_context(tc.tile_pool(name="reuse", bufs=1))
        psum = ctx.enter_context(tc.psum_pool(name="psum", bufs=1))

        offsets = keep.tile([P, S // 16], U16, name="offsets")
        nc.sync.dma_start(offsets[:], offs)

        h_rows = hT.rearrange("(p j) t -> p j t", j=PACK)
        h_raw0 = keep.tile([P, PACK, HALF], F32, name="h_raw0")
        nc.sync.dma_start(out=h_raw0[:], in_=h_rows[:, :, 0:HALF])

        one = reuse.tile([P, 32], F32, name="one", offset=12352, align_bytes=64)
        warm = keep.tile([P, 2], F32, name="warm")
        nc.vector.memset(one[:, 0:1], 1.0)
        nc.scalar.activation(warm[:, 0:1], one[:, 0:1], ACT.Ln)

        scale_table = keep.tile([P, T], U8, name="scale_table")
        nc.vector.memset(scale_table[:].bitcast(I32), 0)

        def load_scales(queue, q):
            queue.dma_start(out=scale_table[32 * q : 32 * q + 4, :].bitcast(I32), in_=x_scales[0, 4 * q : 4 * q + 4, :].bitcast(I32))

        for q in range(4):
            load_scales(nc.sync, q)

        item_table = reuse.tile([P, T + 16], F32, name="item_table", offset=0, align_bytes=64)
        nc.vector.memset(item_table[:].bitcast(I32), 0)
        nc.sync.dma_start(out=item_table[ROW_A : ROW_B + 1 : ROW_B - ROW_A, 0:T], in_=guess[0:2, :])
        nc.sync.dma_start(out=item_table[ROW_D : ROW_D + 1, 0:T], in_=diff[0:1, :])

        ln_scale = keep.tile([P, 1], F32, name="ln_scale")
        ln_bias = keep.tile([P, 1], F32, name="ln_bias")
        nc.gpsimd.memset(ln_scale[0:32, :], 1.0)
        nc.gpsimd.memset(ln_scale[32:64, :], -99.0)
        nc.gpsimd.memset(ln_scale[64:P, :], 0.0)
        nc.gpsimd.memset(ln_bias[0:32, :], LN_FLOOR)
        nc.gpsimd.memset(ln_bias[32:64, :], 100.0)
        nc.vector.tensor_tensor(ln_bias[64:P, :], one[64:P, 0:1], item_table[64:P, T : T + 1], ALU.add)

        word_table = reuse.tile([P, T], U32, name="word_table", offset=12416, align_bytes=64)
        nc.sync.dma_start(out=word_table[:].bitcast(I32), in_=x_words[0].rearrange("p n t -> p (n t)").bitcast(I32))
        h_raw1 = reuse.tile([P, PACK, HALF], F32, name="h_raw1", offset=8320, align_bytes=64)
        nc.sync.dma_start(out=h_raw1[:], in_=h_rows[:, :, HALF:V])

        ident = keep.tile([P, P], F32, name="ident")
        make_identity(nc, ident[:])

        def list_half(h):
            return offsets[:, h * (HALF // 16) : (h + 1) * (HALF // 16)]

        picked = [keep.tile([P, HALF], F32, name=f"picked{h}") for h in range(2)]
        logs = [keep.tile([P, HALF], F32, name=f"logs{h}") for h in range(2)]
        turned = [psum.tile([P, 2, 2, P], F32, name=f"turned{h}", tag="sums", bufs=4) for h in range(2)]
        for h in range(2):
            nc.vector.tensor_copy(picked[h][:], item_table[:, 0:T].indirect(list_half(h)))
            nc.scalar.activation(logs[h][:], picked[h][:], ACT.Ln, bias=ln_bias[:], scale=ln_scale[:])
            for i, src in enumerate((picked[h], logs[h])):
                for c in range(2):
                    nc.tensor.transpose(turned[h][:, i, c, :], src[:, c * P : (c + 1) * P], ident[:])
        nc.scalar.activation(warm[:, 1:2], logs[1][:, 0:1], ACT.Tanh)

        h_codes = reuse.tile([P, V], U32, name="h_codes", offset=2560, align_bytes=64)
        h_scales = keep.tile([P, V], U8, name="h_scales", align_bytes=64)
        x_codes = [reuse.tile([P, HALF], U32, name=f"x_codes{h}", offset=1024 * h, align_bytes=64) for h in range(2)]
        x_bytes = [reuse.tile([P, HALF], U8, name=f"x_bytes{h}", offset=(2048, 12416)[h], align_bytes=64) for h in range(2)]
        h_bf0 = keep.tile([P, HALF, PACK], BF16, name="h_bf0", align_bytes=64)
        h_bf1 = keep.tile([P, HALF, PACK], BF16, name="h_bf1", align_bytes=64)
        h_bf = [h_bf0, h_bf1]
        h_raw = [h_raw0, h_raw1]

        def round_h(h):
            nc.vector.tensor_copy(
                out=h_bf[h][:].rearrange("p (c i) j -> p c j i", i=4),
                in_=h_raw[h][:].rearrange("p j (c i) -> p c j i", i=4),
            )

        def quantize_h(h):
            cols = slice(h * HALF, (h + 1) * HALF)
            nc.vector.quantize_mx(
                out=h_codes[:, cols].bitcast(FP8X4), scales=h_scales[:, cols], in_=h_bf[h][:].rearrange("p w j -> p (w j)")
            )

        def gather_scales(h):
            nc.vector.tensor_copy(x_bytes[h][:], scale_table[:].indirect(list_half(h)))

        def gather_words(h):
            nc.vector.tensor_copy(x_codes[h][:], word_table[:].indirect(list_half(h)))

        bias_n = [keep.tile([P, 2], F32, name="bias_n0"), reuse.tile([P, 2], F32, name="bias_n1", offset=12672, align_bytes=64)]
        bias_ab = [keep.tile([P, 2, 2], F32, name="bias_ab0"), reuse.tile([P, 2, 2], F32, name="bias_ab1", offset=12736, align_bytes=64)]

        def biases(h):
            nc.vector.tensor_scalar(bias_n[h][:], turned[h][:, 0, :, ROW_D], HALF_SLOPE, None, ALU.mult)
            nc.vector.scalar_tensor_tensor(
                bias_ab[h][:], turned[h][:, 1, :, ROW_A : ROW_B + 1 : ROW_B - ROW_A], -0.5,
                bias_n[h][:].unsqueeze(2).to_broadcast([P, 2, 2]), ALU.mult, ALU.subtract,
            )

        round_h(0)
        quantize_h(0)
        gather_scales(0)
        biases(0)
        gather_words(0)
        gather_words(1)
        gather_scales(1)
        biases(1)
        round_h(1)
        quantize_h(1)

        out_rows = out.rearrange("(c p) j -> p c j", p=P)

        def products(units):
            bank = psum.tile([P, 2 * HALF], F32, name="score", tag="score", bufs=4)
            views = []
            for i, u in enumerate(units):
                b, t0, n = UNITS[u]
                items = slice((b % 2) * P, (b % 2 + 1) * P)
                view = bank[:, i * HALF : i * HALF + n]
                nc.tensor.matmul_mx(
                    out=view,
                    lhsT=x_codes[b // 2][:, items].bitcast(FP8X4),
                    lhsT_scale=x_bytes[b // 2][:, items],
                    rhs=h_codes[:, t0 : t0 + n].bitcast(FP8X4),
                    rhs_scale=h_scales[:, t0 : t0 + n],
                    start=True,
                    stop=True,
                )
                views.append(view)
            return views

        def turn(dst, src, chunks, start, stop):
            for c in range(chunks):
                nc.tensor.matmul(
                    dst[:, c, :], src[:, c * P : (c + 1) * P], ident[:],
                    start=start and c == 0, stop=stop and c == chunks - 1, is_transpose=True,
                )

        def tanh_tiles(name, n):
            return [keep.tile([P, n], F32, name=f"tanh_{kind}{name}") for kind in ("n", "b", "a")]

        def store(result, b, t0, chunks):
            nc.sync.dma_start(out=out_rows[:, t0 // P : t0 // P + chunks, b * P : (b + 1) * P], in_=result[:])

        def sums_on_tensor(name, b, t0, score, last):
            n = score.shape[1]
            chunks = n // P
            tanh_n, tanh_b, tanh_a = tanh_tiles(name, n)
            if last:
                bank_b = psum.tile([P, chunks, P], F32, name="bank_b", tag="score", bufs=4)
                bank_a = psum.tile([P, chunks, P], F32, name="bank_a", tag="sums", bufs=4)
                sum_b, sum_a = bank_b[:], bank_a[:]
            else:
                bank = psum.tile([P, 2, chunks, P], F32, name="bank", tag="sums", bufs=4)
                sum_b, sum_a = bank[:, 0, :, :], bank[:, 1, :, :]
            nc.scalar.activation(tanh_n[:], score, ACT.Tanh, bias=bias_n[b // 2][:, b % 2 : b % 2 + 1], scale=-HALF_SLOPE)
            turn(sum_b, tanh_n, chunks, True, False)
            turn(sum_a, tanh_n, chunks, last, False)
            nc.scalar.activation(tanh_b[:], score, ACT.Tanh, bias=bias_ab[b // 2][:, b % 2, 1:2], scale=HALF_SLOPE)
            turn(sum_b, tanh_b, chunks, False, last)
            nc.scalar.activation(tanh_a[:], score, ACT.Tanh, bias=bias_ab[b // 2][:, b % 2, 0:1], scale=HALF_SLOPE)
            turn(sum_a, tanh_a, chunks, False, True)

            def finish():
                factor_b = keep.tile([P, chunks, P], F32, name=f"factor_b{name}")
                if last:
                    nc.scalar.copy(factor_b[:], sum_b)
                else:
                    nc.vector.tensor_copy(factor_b[:], sum_b)
                result = keep.tile([P, chunks, P], F32, name=f"result{name}")
                nc.vector.scalar_tensor_tensor(result[:], sum_a, OUT_FACTOR, factor_b[:], ALU.mult, ALU.mult)
                store(result, b, t0, chunks)

            return finish

        def sums_shared(name, b, t0, score):
            n = score.shape[1]
            chunks = n // P
            tanh_n, tanh_b, tanh_a = tanh_tiles(name, n)
            sum_items = keep.tile([P, n], F32, name=f"sum_items{name}")
            bank = psum.tile([P, 2, chunks, P], F32, name="bank", tag="sums", bufs=4)
            sum_b, sum_a = bank[:, 0, :, :], bank[:, 1, :, :]
            nc.scalar.activation(tanh_n[:], score, ACT.Tanh, bias=bias_n[b // 2][:, b % 2 : b % 2 + 1], scale=-HALF_SLOPE)
            turn(sum_a, tanh_n, chunks, True, False)
            nc.scalar.activation(tanh_b[:], score, ACT.Tanh, bias=bias_ab[b // 2][:, b % 2, 1:2], scale=HALF_SLOPE)
            nc.gpsimd.tensor_tensor(sum_items[:], tanh_b[:], tanh_n[:], ALU.add)
            nc.scalar.activation(tanh_a[:], score, ACT.Tanh, bias=bias_ab[b // 2][:, b % 2, 0:1], scale=HALF_SLOPE)
            turn(sum_a, tanh_a, chunks, False, False)
            turn(sum_b, sum_items, chunks, False, True)

            def finish():
                factor_b = keep.tile([P, chunks, P], F32, name=f"factor_b{name}")
                nc.vector.tensor_copy(factor_b[:], sum_b)
                result = keep.tile([P, chunks, P], F32, name=f"result{name}")
                nc.vector.scalar_tensor_tensor(result[:], sum_a, OUT_FACTOR, factor_b[:], ALU.mult, ALU.mult)
                store(result, b, t0, chunks)

            return finish

        def sums_on_vector(name, b, t0, score, between, copy_on_scalar):
            n = score.shape[1]
            chunks = n // P
            tanh_n, tanh_b, tanh_a = tanh_tiles(name, n)
            sum_b = keep.tile([P, n], F32, name=f"sum_b{name}")
            sum_a = keep.tile([P, n], F32, name=f"sum_a{name}")
            info = keep.tile([P, n], F32, name=f"info{name}")
            nc.scalar.activation(tanh_n[:], score, ACT.Tanh, bias=bias_n[b // 2][:, b % 2 : b % 2 + 1], scale=-HALF_SLOPE)
            nc.scalar.activation(tanh_b[:], score, ACT.Tanh, bias=bias_ab[b // 2][:, b % 2, 1:2], scale=HALF_SLOPE)
            nc.scalar.activation(tanh_a[:], score, ACT.Tanh, bias=bias_ab[b // 2][:, b % 2, 0:1], scale=HALF_SLOPE)
            nc.vector.tensor_tensor(sum_b[:], tanh_b[:], tanh_n[:], ALU.add)
            nc.vector.tensor_tensor(sum_a[:], tanh_a[:], tanh_n[:], ALU.add)
            between()
            nc.vector.scalar_tensor_tensor(info[:], sum_a[:], OUT_FACTOR, sum_b[:], ALU.mult, ALU.mult)
            bank = psum.tile([P, chunks, P], F32, name="bank", tag="sums", bufs=4)
            turn(bank, info, chunks, True, True)

            def finish():
                result = keep.tile([P, chunks, P], F32, name=f"result{name}")
                if copy_on_scalar:
                    nc.scalar.copy(result[:], bank[:])
                else:
                    nc.vector.tensor_copy(result[:], bank[:])
                store(result, b, t0, chunks)

            return finish

        scores = products([0]) + products([1])
        f0 = sums_on_tensor("0", 0, 0, scores[0], False)
        scores = scores + products([2, 3])
        f1 = sums_on_tensor("1", 1, 0, scores[1], False)
        f0()
        scores = scores + products([4, 5]) + products([6, 7])
        f2 = sums_on_tensor("2", 2, 0, scores[2], False)
        f1()
        f3 = sums_shared("3", 3, 0, scores[3])
        f2()
        f4 = sums_shared("4", 0, HALF, scores[4])
        f3()
        f5 = sums_shared("5", 1, HALF, scores[5])
        f4()
        f6 = sums_shared("6", 2, HALF, scores[6])
        f5()
        f7a = sums_on_tensor("7a", 3, HALF, scores[7][:, 0:P], True)
        f6()
        f7b = sums_on_tensor("7b", 3, HALF + P, scores[7][:, P:HALF], True)
        f7a()
        f7b()
